import numpy as np
import ml_dtypes


def mxq(x, axis, fmt="e4m3"):
    dtype, down = {"e4m3": (ml_dtypes.float8_e4m3fn, 7), "e5m2": (ml_dtypes.float8_e5m2, 14)}[fmt]
    v = np.moveaxis(np.asarray(x, np.float32).astype(ml_dtypes.bfloat16).astype(np.float64), axis, -1)
    blocks = v.reshape(v.shape[:-1] + (-1, 32))
    amax = np.abs(blocks).max(-1, keepdims=True)
    byte = np.maximum(np.where(amax > 0, np.frexp(amax)[1] - 1 + 127, 0) - down, 1)
    scale = np.exp2(byte - 127.0)
    codes = (blocks / scale).astype(np.float32).astype(dtype).astype(np.float64)
    return np.moveaxis((codes * scale).reshape(v.shape), -1, axis)


WIDE = False


def mx_kscale(k):
    if not WIDE:
        return np.ones(k)
    levels = np.array([10, -10, 5, -5, 0])
    if k % 512:
        return np.exp2(np.random.permutation(np.resize(levels, k // 32))).repeat(32)
    a = np.empty((k // 512, 16))
    for p in range(k // 512):
        a[p, :8] = np.random.permutation(np.resize(levels, 8))
        for g in range(8):
            far = levels[np.abs(levels - a[p, g]) >= 10]
            a[p, g + 8] = far[np.random.randint(len(far))]
    return np.exp2(a.ravel()).repeat(32)


def f64(x):
    return np.asarray(x).astype(np.float64)


def striped(idx):
    return np.tile(idx.reshape(-1, 16).T, (8, 1)).astype(np.uint16)


def unstriped(offs):
    return offs[:16].T.reshape(-1).astype(np.int64)


def silu(v):
    return v / (1.0 + np.exp(-np.maximum(v, -700.0)))


K, T, D, S, V, H, N = 512, 2048, 2, 1024, 512, 512, 128
P = 2 ** 7


def setup_inputs():
    n = np.random.standard_normal
    s = mx_kscale(K)[:, None]
    u = mx_kscale(H)
    q = np.random.permutation(S)
    return {
        "xT": (n((K, T)) * s).astype(np.float32),
        "w1": (n((K, H)) / np.sqrt(K) / s * u).astype(np.float32),
        "w2": (n((H, N)) / np.sqrt(H) / u[:, None]).astype(np.float32),
        "gate": np.tile(np.random.uniform(0.2, 1.0, (D, 1, V)) / np.sqrt(D), (1, P, 1)).astype(np.float32),
        "offs": striped(np.random.permutation(T)[:S]),
        "pos1": striped(q[:V]),
        "pos2": striped(q[V:]),
    }


def reference(xT, w1, w2, gate, offs, pos1, pos2):
    h = silu(mxq(f64(w1), 0, "e4m3").T @ mxq(f64(xT)[:, unstriped(offs)], 0, "e4m3"))
    z = sum(f64(gate)[d, :1] * h[:, unstriped(p)] for d, p in enumerate((pos1, pos2)))
    return mxq(f64(w2), 0, "e4m3").T @ mxq(z, 0, "e4m3")

@@ -1,0 +1,176 @@
+from contextlib import ExitStack
+
+import concourse.mybir as mybir
+
+K, T, D, S, V, H, N = 512, 2048, 2, 1024, 512, 512, 128
+FLOPS = 2 * K * H * S + 2 * H * N * V
+
+F32 = mybir.dt.float32
+BF16 = mybir.dt.bfloat16
+U32 = mybir.dt.uint32
+U16 = mybir.dt.uint16
+U8 = mybir.dt.uint8
+FP8X4 = mybir.dt.float8_e4m3fn_x4
+COPY = mybir.ActivationFunctionType.Copy
+SILU = mybir.ActivationFunctionType.Silu
+ADD = mybir.AluOpType.add
+MULT = mybir.AluOpType.mult
+
+P = 128
+J = 4
+
+
+def tile_picked_sage_silu_e_kernel(tc, xT, w1, w2, gate, offs, pos1, pos2, out):
+    nc = tc.nc
+    with ExitStack() as ctx:
+        keep = ctx.enter_context(tc.tile_pool(name="keep", bufs=1))
+        psum = ctx.enter_context(tc.psum_pool(name="psum", bufs=1))
+
+        offs_sb = keep.tile([P, S // 16], U16, name="offs_sb")
+        pos1_sb = keep.tile([P, V // 16], U16, name="pos1_sb")
+        pos2_sb = keep.tile([P, V // 16], U16, name="pos2_sb")
+        gate_sb = keep.tile([P, D, V], F32, name="gate_sb")
+        w1_raw = keep.tile([P, J, H], F32, name="w1_raw")
+        w2_raw = keep.tile([P, J, N], F32, name="w2_raw")
+        w1_b = keep.tile([P, H * J], BF16, name="w1_b", align_bytes=64)
+        w2_b = keep.tile([P, N * J], BF16, name="w2_b", align_bytes=64)
+        w1_c = keep.tile([P, H], U32, name="w1_c", align_bytes=64)
+        w1_s = keep.tile([P, H], U8, name="w1_s", align_bytes=64)
+        w2_c = keep.tile([P, N], U32, name="w2_c", align_bytes=64)
+        w2_s = keep.tile([P, N], U8, name="w2_s", align_bytes=64)
+        xb = [keep.tile([P, T * 2], BF16, name=f"xb{u}", align_bytes=64) for u in range(2)]
+        grouped = keep.tile([P, S * J], BF16, name="grouped", align_bytes=64)
+        x_c = keep.tile([P, S], U32, name="x_c", align_bytes=64)
+        x_s = keep.tile([P, S], U8, name="x_s", align_bytes=64)
+        h = [keep.tile([P, S], F32, name=f"h{t}", align_bytes=64) for t in range(J)]
+        m = [keep.tile([P, J, V], F32, name=f"m{d}", align_bytes=64) for d in range(D)]
+        z_b = keep.tile([P, V * J], BF16, name="z_b", align_bytes=64)
+        z_c = keep.tile([P, V], U32, name="z_c", align_bytes=64)
+        z_s = keep.tile([P, V], U8, name="z_s", align_bytes=64)
+        o_sb = keep.tile([P, V], F32, name="o_sb", align_bytes=64)
+        warm = keep.tile([P, 1], F32, name="warm")
+
+        nc.vector.memset(warm[:], 0.0)
+        nc.scalar.activation(warm[:], warm[:], SILU)
+
+        x_view = xT.rearrange("(p u e) t -> p u e t", u=2, e=2)
+        chunks = [(0, 0, 1024), (0, 1024, 1024), (1, 0, 1024), (1, 1024, 512), (1, 1536, 512)]
+        raws = []
+        for i, (u, c0, n) in enumerate(chunks):
+            raw = keep.tile([P, 2, n], F32, name=f"x_raw{i}", align_bytes=64)
+            nc.sync.dma_start(out=raw[:], in_=x_view[:, u, :, c0 : c0 + n])
+            raws.append(raw)
+            if i == 0:
+                nc.sync.dma_start(out=offs_sb[:], in_=offs)
+        w1_view = w1.rearrange("(p j) c -> p j c", j=J)
+        for c0 in (0, H // 2):
+            nc.sync.dma_start(out=w1_raw[:, :, c0 : c0 + H // 2], in_=w1_view[:, :, c0 : c0 + H // 2])
+        nc.sync.dma_start(out=w2_raw[:], in_=w2.rearrange("(p j) n -> p j n", j=J))
+        nc.sync.dma_start(out=pos1_sb[:], in_=pos1)
+        nc.sync.dma_start(out=gate_sb[:], in_=gate.rearrange("d p v -> p d v"))
+        nc.sync.dma_start(out=pos2_sb[:], in_=pos2)
+
+        g_words = grouped[:].bitcast(U32).rearrange("p (s u) -> p s u", u=2)
+
+        def round_cols(i, a, n, on_vector):
+            u, c0 = chunks[i][:2]
+            dst = xb[u][:, 2 * (c0 + a) : 2 * (c0 + a + n)].rearrange("p (t e) -> p t e", e=2)
+            src = raws[i][:, :, a : a + n].rearrange("p e t -> p t e")
+            if on_vector:
+                nc.vector.tensor_copy(out=dst, in_=src)
+            else:
+                nc.scalar.activation(dst, src, COPY)
+
+        def gather(u, s0, n):
+            nc.vector.tensor_copy(
+                out=g_words[:, s0 : s0 + n, u],
+                in_=xb[u][:].bitcast(U32).indirect(offs_sb[:, s0 // 16 : (s0 + n) // 16]),
+            )
+
+        def quantize(codes, scales, src, c0, n):
+            nc.vector.quantize_mx(
+                out=codes[:, c0 : c0 + n].bitcast(FP8X4),
+                scales=scales[:, c0 : c0 + n],
+                in_=src[:, J * c0 : J * (c0 + n)],
+            )
+
+        def split(i, n_vector):
+            n = chunks[i][2]
+            if n_vector:
+                round_cols(i, 0, n_vector, True)
+            round_cols(i, n_vector, n - n_vector, False)
+
+        split(0, 512)
+        split(1, 512)
+        gather(0, 0, S)
+        split(2, 512)
+        split(3, 320)
+        split(4, 320)
+        gather(1, 0, 512)
+        gather(1, 512, 256)
+        gather(1, 768, 256)
+
+        w1_dst = w1_b[:].rearrange("p (t m j) -> p m t j", t=J, j=J)
+        w1_src = w1_raw[:].rearrange("p j (m t) -> p m t j", t=J)
+        for c0 in (0, P // 2):
+            nc.scalar.activation(w1_dst[:, c0 : c0 + P // 2], w1_src[:, c0 : c0 + P // 2], COPY)
+        nc.scalar.activation(
+            w2_b[:].rearrange("p (n j) -> p n j", j=J), w2_raw[:].rearrange("p j n -> p n j"), COPY
+        )
+        quantize(x_c, x_s, grouped, 0, 512)
+        quantize(w1_c, w1_s, w1_b, 0, P)
+        quantize(x_c, x_s, grouped, 512, 256)
+        quantize(x_c, x_s, grouped, 768, 256)
+        for t in range(1, J):
+            quantize(w1_c, w1_s, w1_b, P * t, P)
+        quantize(w2_c, w2_s, w2_b, 0, N)
+
+        banks = [psum.tile([P, 512], F32, name=f"bank{i}") for i in range(8)]
+        for t in range(J):
+            slices = [(0, 0, 512), (1, 512, 256), (1, 768, 256)] if t == 0 else [(0, 0, 512), (1, 512, 512)]
+            for b, s0, n in slices:
+                sl = slice(s0, s0 + n)
+                acc = banks[2 * t + b][:, s0 % 512 : s0 % 512 + n]
+                nc.tensor.matmul_mx(
+                    out=acc,
+                    lhsT=w1_c[:, P * t : P * t + P].bitcast(FP8X4),
+                    lhsT_scale=w1_s[:, P * t : P * t + P],
+                    rhs=x_c[:, sl].bitcast(FP8X4),
+                    rhs_scale=x_s[:, sl],
+                    start=True,
+                    stop=True,
+                )
+                nc.scalar.activation(h[t][:, sl], acc, SILU)
+
+        for t in range(J):
+            for d, pos in enumerate((pos1_sb, pos2_sb)):
+                nc.vector.tensor_tensor(m[d][:, t, :], h[t][:].indirect(pos[:]), gate_sb[:, d, :], MULT)
+
+        def add(v0, n):
+            pat = "p t (c i) -> p c t i"
+            nc.vector.tensor_tensor(
+                z_b[:, J * v0 : J * (v0 + n)].rearrange("p (c i t) -> p c t i", t=J, i=4),
+                m[0][:, :, v0 : v0 + n].rearrange(pat, i=4),
+                m[1][:, :, v0 : v0 + n].rearrange(pat, i=4),
+                ADD,
+            )
+
+        half_v = V // 2
+        add(0, half_v)
+        add(half_v, half_v)
+        for i in range(2):
+            quantize(z_c, z_s, z_b, i * half_v, half_v)
+        for i in range(2):
+            sl = slice(i * half_v, (i + 1) * half_v)
+            acc = banks[i]
+            nc.tensor.matmul_mx(
+                out=acc[:, :half_v],
+                lhsT=w2_c[:].bitcast(FP8X4),
+                lhsT_scale=w2_s[:],
+                rhs=z_c[:, sl].bitcast(FP8X4),
+                rhs_scale=z_s[:, sl],
+                start=True,
+                stop=True,
+            )
+            nc.scalar.copy(o_sb[:, sl], acc[:, :half_v])
+            nc.sync.dma_start(out=out[:, sl], in_=o_sb[:, sl])

@@ -32,16 +32,16 @@ def tile_picked_sage_silu_e_kernel(tc, xT, w1, w2, gate, offs, pos1, pos2, out):
         gate_sb = keep.tile([P, D, V], F32, name="gate_sb")
         w1_raw = keep.tile([P, J, H], F32, name="w1_raw")
         w2_raw = keep.tile([P, J, N], F32, name="w2_raw")
-        w1_b = keep.tile([P, H * J], BF16, name="w1_b", align_bytes=64)
-        w2_b = keep.tile([P, N * J], BF16, name="w2_b", align_bytes=64)
         w1_c = keep.tile([P, H], U32, name="w1_c", align_bytes=64)
         w1_s = keep.tile([P, H], U8, name="w1_s", align_bytes=64)
         w2_c = keep.tile([P, N], U32, name="w2_c", align_bytes=64)
         w2_s = keep.tile([P, N], U8, name="w2_s", align_bytes=64)
         xb = [keep.tile([P, T * 2], BF16, name=f"xb{u}", align_bytes=64) for u in range(2)]
-        grouped = keep.tile([P, S * J], BF16, name="grouped", align_bytes=64)
-        x_c = keep.tile([P, S], U32, name="x_c", align_bytes=64)
+        early = keep.tile([P, S * J + P * J], BF16, name="early", tag="stage", align_bytes=64)
+        grouped = early[:, : S * J]
+        x_c = keep.tile([P, 768], U32, name="x_c", align_bytes=64)
         x_s = keep.tile([P, S], U8, name="x_s", align_bytes=64)
+        w1_e0 = keep.tile([P, P * J], BF16, name="w1_e0", tag="first", align_bytes=64)
         h = [keep.tile([P, S], F32, name=f"h{t}", align_bytes=64) for t in range(J)]
         m = [keep.tile([P, J, V], F32, name=f"m{d}", align_bytes=64) for d in range(D)]
         z_b = keep.tile([P, V * J], BF16, name="z_b", align_bytes=64)
@@ -65,12 +65,12 @@ def tile_picked_sage_silu_e_kernel(tc, xT, w1, w2, gate, offs, pos1, pos2, out):
         w1_view = w1.rearrange("(p j) c -> p j c", j=J)
         for c0 in (0, H // 2):
             nc.sync.dma_start(out=w1_raw[:, :, c0 : c0 + H // 2], in_=w1_view[:, :, c0 : c0 + H // 2])
-        nc.sync.dma_start(out=w2_raw[:], in_=w2.rearrange("(p j) n -> p j n", j=J))
         nc.sync.dma_start(out=pos1_sb[:], in_=pos1)
         nc.sync.dma_start(out=gate_sb[:], in_=gate.rearrange("d p v -> p d v"))
+        nc.sync.dma_start(out=w2_raw[:], in_=w2.rearrange("(p j) n -> p j n", j=J))
         nc.sync.dma_start(out=pos2_sb[:], in_=pos2)
 
-        g_words = grouped[:].bitcast(U32).rearrange("p (s u) -> p s u", u=2)
+        g_words = grouped.bitcast(U32).rearrange("p (s u) -> p s u", u=2)
 
         def round_cols(i, a, n, on_vector):
             u, c0 = chunks[i][:2]
@@ -87,11 +87,12 @@ def tile_picked_sage_silu_e_kernel(tc, xT, w1, w2, gate, offs, pos1, pos2, out):
                 in_=xb[u][:].bitcast(U32).indirect(offs_sb[:, s0 // 16 : (s0 + n) // 16]),
             )
 
-        def quantize(codes, scales, src, c0, n):
+        def quantize(codes, scales, src, c0, n, s0=None):
+            s0 = c0 if s0 is None else s0
             nc.vector.quantize_mx(
                 out=codes[:, c0 : c0 + n].bitcast(FP8X4),
                 scales=scales[:, c0 : c0 + n],
-                in_=src[:, J * c0 : J * (c0 + n)],
+                in_=src[:, J * s0 : J * (s0 + n)],
             )
 
         def split(i, n_vector):
@@ -106,42 +107,50 @@ def tile_picked_sage_silu_e_kernel(tc, xT, w1, w2, gate, offs, pos1, pos2, out):
         split(2, 512)
         split(3, 320)
         split(4, 320)
-        gather(1, 0, 512)
-        gather(1, 512, 256)
-        gather(1, 768, 256)
-
-        w1_dst = w1_b[:].rearrange("p (t m j) -> p m t j", t=J, j=J)
         w1_src = w1_raw[:].rearrange("p j (m t) -> p m t j", t=J)
-        for c0 in (0, P // 2):
-            nc.scalar.activation(w1_dst[:, c0 : c0 + P // 2], w1_src[:, c0 : c0 + P // 2], COPY)
-        nc.scalar.activation(
-            w2_b[:].rearrange("p (n j) -> p n j", j=J), w2_raw[:].rearrange("p j n -> p n j"), COPY
-        )
+        w1_e1 = early[:, S * J :]
+        for t, dst in ((0, w1_e0[:]), (1, w1_e1)):
+            for m0 in (0, P // 2):
+                nc.scalar.activation(
+                    dst.rearrange("p (m j) -> p m j", j=J)[:, m0 : m0 + P // 2], w1_src[:, m0 : m0 + P // 2, t], COPY
+                )
+        gather(1, 0, 768)
         quantize(x_c, x_s, grouped, 0, 512)
-        quantize(w1_c, w1_s, w1_b, 0, P)
         quantize(x_c, x_s, grouped, 512, 256)
-        quantize(x_c, x_s, grouped, 768, 256)
-        for t in range(1, J):
-            quantize(w1_c, w1_s, w1_b, P * t, P)
-        quantize(w2_c, w2_s, w2_b, 0, N)
+        quantize(w1_c, w1_s, w1_e0, 0, P)
+        gather(1, 768, 256)
+        x_c2 = keep.tile([P, 256], U32, name="x_c2", tag="first", align_bytes=64)
+        nc.vector.quantize_mx(
+            out=x_c2[:].bitcast(FP8X4), scales=x_s[:, 768:], in_=grouped[:, 768 * J :]
+        )
 
         banks = [psum.tile([P, 512], F32, name=f"bank{i}") for i in range(8)]
-        for t in range(J):
-            slices = [(0, 0, 512), (1, 512, 256), (1, 768, 256)] if t == 0 else [(0, 0, 512), (1, 512, 512)]
-            for b, s0, n in slices:
-                sl = slice(s0, s0 + n)
-                acc = banks[2 * t + b][:, s0 % 512 : s0 % 512 + n]
+
+        def layer1(t):
+            for s0, n in ((0, 512), (512, 256), (768, 256)):
+                codes = x_c[:, s0 : s0 + n] if s0 < 768 else x_c2[:]
                 nc.tensor.matmul_mx(
-                    out=acc,
+                    out=banks[2 * t + s0 // 512][:, s0 % 512 : s0 % 512 + n],
                     lhsT=w1_c[:, P * t : P * t + P].bitcast(FP8X4),
                     lhsT_scale=w1_s[:, P * t : P * t + P],
-                    rhs=x_c[:, sl].bitcast(FP8X4),
-                    rhs_scale=x_s[:, sl],
+                    rhs=codes.bitcast(FP8X4),
+                    rhs_scale=x_s[:, s0 : s0 + n],
                     start=True,
                     stop=True,
                 )
-                nc.scalar.activation(h[t][:, sl], acc, SILU)
+            for half in range(2):
+                nc.scalar.activation(h[t][:, half * 512 : half * 512 + 512], banks[2 * t + half][:], SILU)
 
+        layer1(0)
+        quantize(w1_c, w1_s, w1_e1, P, P, 0)
+        late = keep.tile([P, 2 * P * J + N * J], BF16, name="late", tag="stage", align_bytes=64)
+        w1_late = late[:, : 2 * P * J]
+        w2_late = late[:, 2 * P * J :]
+        nc.vector.tensor_copy(out=w1_late.rearrange("p (t m j) -> p m t j", t=2, j=J), in_=w1_src[:, :, 2:])
+        quantize(w1_c, w1_s, w1_late, 2 * P, 2 * P, 0)
+        nc.vector.tensor_copy(out=w2_late.rearrange("p (n j) -> p n j", j=J), in_=w2_raw[:].rearrange("p j n -> p n j"))
+        for t in range(1, J):
+            layer1(t)
         for t in range(J):
             for d, pos in enumerate((pos1_sb, pos2_sb)):
                 nc.vector.tensor_tensor(m[d][:, t, :], h[t][:].indirect(pos[:]), gate_sb[:, d, :], MULT)
@@ -156,6 +165,7 @@ def tile_picked_sage_silu_e_kernel(tc, xT, w1, w2, gate, offs, pos1, pos2, out):
             )
 
         half_v = V // 2
+        quantize(w2_c, w2_s, w2_late, 0, N)
         add(0, half_v)
         add(half_v, half_v)
         for i in range(2):

from contextlib import ExitStack

import concourse.mybir as mybir

K, T, D, S, V, H, N = 512, 2048, 2, 1024, 512, 512, 128
FLOPS = 2 * K * H * S + 2 * H * N * V

F32 = mybir.dt.float32
BF16 = mybir.dt.bfloat16
U32 = mybir.dt.uint32
U16 = mybir.dt.uint16
U8 = mybir.dt.uint8
FP8X4 = mybir.dt.float8_e4m3fn_x4
COPY = mybir.ActivationFunctionType.Copy
SILU = mybir.ActivationFunctionType.Silu
ADD = mybir.AluOpType.add
MULT = mybir.AluOpType.mult

P = 128
J = 4


def tile_picked_sage_silu_e_kernel(tc, xT, w1, w2, gate, offs, pos1, pos2, out):
    nc = tc.nc
    with ExitStack() as ctx:
        keep = ctx.enter_context(tc.tile_pool(name="keep", bufs=1))
        psum = ctx.enter_context(tc.psum_pool(name="psum", bufs=1))

        offs_sb = keep.tile([P, S // 16], U16, name="offs_sb")
        pos1_sb = keep.tile([P, V // 16], U16, name="pos1_sb")
        pos2_sb = keep.tile([P, V // 16], U16, name="pos2_sb")
        gate_sb = keep.tile([P, D, V], F32, name="gate_sb")
        w1_raw = keep.tile([P, J, H], F32, name="w1_raw")
        w2_raw = keep.tile([P, J, N], F32, name="w2_raw")
        w1_c = keep.tile([P, H], U32, name="w1_c", align_bytes=64)
        w1_s = keep.tile([P, H], U8, name="w1_s", align_bytes=64)
        w2_c = keep.tile([P, N], U32, name="w2_c", align_bytes=64)
        w2_s = keep.tile([P, N], U8, name="w2_s", align_bytes=64)
        xb = [keep.tile([P, T * 2], BF16, name=f"xb{u}", align_bytes=64) for u in range(2)]
        early = keep.tile([P, S * J + P * J], BF16, name="early", tag="stage", align_bytes=64)
        grouped = early[:, : S * J]
        x_c = keep.tile([P, 768], U32, name="x_c", align_bytes=64)
        x_s = keep.tile([P, S], U8, name="x_s", align_bytes=64)
        w1_e0 = keep.tile([P, P * J], BF16, name="w1_e0", tag="first", align_bytes=64)
        h = [keep.tile([P, S], F32, name=f"h{t}", align_bytes=64) for t in range(J)]
        m = [keep.tile([P, J, V], F32, name=f"m{d}", align_bytes=64) for d in range(D)]
        z_b = keep.tile([P, V * J], BF16, name="z_b", align_bytes=64)
        z_c = keep.tile([P, V], U32, name="z_c", align_bytes=64)
        z_s = keep.tile([P, V], U8, name="z_s", align_bytes=64)
        o_sb = keep.tile([P, V], F32, name="o_sb", align_bytes=64)
        warm = keep.tile([P, 1], F32, name="warm")

        nc.vector.memset(warm[:], 0.0)
        nc.scalar.activation(warm[:], warm[:], SILU)

        x_view = xT.rearrange("(p u e) t -> p u e t", u=2, e=2)
        chunks = [(0, 0, 1024), (0, 1024, 1024), (1, 0, 1024), (1, 1024, 512), (1, 1536, 512)]
        raws = []
        for i, (u, c0, n) in enumerate(chunks):
            raw = keep.tile([P, 2, n], F32, name=f"x_raw{i}", align_bytes=64)
            nc.sync.dma_start(out=raw[:], in_=x_view[:, u, :, c0 : c0 + n])
            raws.append(raw)
            if i == 0:
                nc.sync.dma_start(out=offs_sb[:], in_=offs)
        w1_view = w1.rearrange("(p j) c -> p j c", j=J)
        for c0 in (0, H // 2):
            nc.sync.dma_start(out=w1_raw[:, :, c0 : c0 + H // 2], in_=w1_view[:, :, c0 : c0 + H // 2])
        nc.sync.dma_start(out=pos1_sb[:], in_=pos1)
        nc.sync.dma_start(out=gate_sb[:], in_=gate.rearrange("d p v -> p d v"))
        nc.sync.dma_start(out=w2_raw[:], in_=w2.rearrange("(p j) n -> p j n", j=J))
        nc.sync.dma_start(out=pos2_sb[:], in_=pos2)

        g_words = grouped.bitcast(U32).rearrange("p (s u) -> p s u", u=2)

        def round_cols(i, a, n, on_vector):
            u, c0 = chunks[i][:2]
            dst = xb[u][:, 2 * (c0 + a) : 2 * (c0 + a + n)].rearrange("p (t e) -> p t e", e=2)
            src = raws[i][:, :, a : a + n].rearrange("p e t -> p t e")
            if on_vector:
                nc.vector.tensor_copy(out=dst, in_=src)
            else:
                nc.scalar.activation(dst, src, COPY)

        def gather(u, s0, n):
            nc.vector.tensor_copy(
                out=g_words[:, s0 : s0 + n, u],
                in_=xb[u][:].bitcast(U32).indirect(offs_sb[:, s0 // 16 : (s0 + n) // 16]),
            )

        def quantize(codes, scales, src, c0, n, s0=None):
            s0 = c0 if s0 is None else s0
            nc.vector.quantize_mx(
                out=codes[:, c0 : c0 + n].bitcast(FP8X4),
                scales=scales[:, c0 : c0 + n],
                in_=src[:, J * s0 : J * (s0 + n)],
            )

        def split(i, n_vector):
            n = chunks[i][2]
            if n_vector:
                round_cols(i, 0, n_vector, True)
            round_cols(i, n_vector, n - n_vector, False)

        split(0, 512)
        split(1, 512)
        gather(0, 0, S)
        split(2, 512)
        split(3, 320)
        split(4, 320)
        w1_src = w1_raw[:].rearrange("p j (m t) -> p m t j", t=J)
        w1_e1 = early[:, S * J :]
        for t, dst in ((0, w1_e0[:]), (1, w1_e1)):
            for m0 in (0, P // 2):
                nc.scalar.activation(
                    dst.rearrange("p (m j) -> p m j", j=J)[:, m0 : m0 + P // 2], w1_src[:, m0 : m0 + P // 2, t], COPY
                )
        gather(1, 0, 768)
        quantize(x_c, x_s, grouped, 0, 512)
        quantize(x_c, x_s, grouped, 512, 256)
        quantize(w1_c, w1_s, w1_e0, 0, P)
        gather(1, 768, 256)
        x_c2 = keep.tile([P, 256], U32, name="x_c2", tag="first", align_bytes=64)
        nc.vector.quantize_mx(
            out=x_c2[:].bitcast(FP8X4), scales=x_s[:, 768:], in_=grouped[:, 768 * J :]
        )

        banks = [psum.tile([P, 512], F32, name=f"bank{i}") for i in range(8)]

        def layer1(t):
            for s0, n in ((0, 512), (512, 256), (768, 256)):
                codes = x_c[:, s0 : s0 + n] if s0 < 768 else x_c2[:]
                nc.tensor.matmul_mx(
                    out=banks[2 * t + s0 // 512][:, s0 % 512 : s0 % 512 + n],
                    lhsT=w1_c[:, P * t : P * t + P].bitcast(FP8X4),
                    lhsT_scale=w1_s[:, P * t : P * t + P],
                    rhs=codes.bitcast(FP8X4),
                    rhs_scale=x_s[:, s0 : s0 + n],
                    start=True,
                    stop=True,
                )
            for half in range(2):
                nc.scalar.activation(h[t][:, half * 512 : half * 512 + 512], banks[2 * t + half][:], SILU)

        layer1(0)
        quantize(w1_c, w1_s, w1_e1, P, P, 0)
        late = keep.tile([P, 2 * P * J + N * J], BF16, name="late", tag="stage", align_bytes=64)
        w1_late = late[:, : 2 * P * J]
        w2_late = late[:, 2 * P * J :]
        nc.vector.tensor_copy(out=w1_late.rearrange("p (t m j) -> p m t j", t=2, j=J), in_=w1_src[:, :, 2:])
        quantize(w1_c, w1_s, w1_late, 2 * P, 2 * P, 0)
        nc.vector.tensor_copy(out=w2_late.rearrange("p (n j) -> p n j", j=J), in_=w2_raw[:].rearrange("p j n -> p n j"))
        for t in range(1, J):
            layer1(t)
        for t in range(J):
            for d, pos in enumerate((pos1_sb, pos2_sb)):
                nc.vector.tensor_tensor(m[d][:, t, :], h[t][:].indirect(pos[:]), gate_sb[:, d, :], MULT)

        def add(v0, n):
            pat = "p t (c i) -> p c t i"
            nc.vector.tensor_tensor(
                z_b[:, J * v0 : J * (v0 + n)].rearrange("p (c i t) -> p c t i", t=J, i=4),
                m[0][:, :, v0 : v0 + n].rearrange(pat, i=4),
                m[1][:, :, v0 : v0 + n].rearrange(pat, i=4),
                ADD,
            )

        half_v = V // 2
        quantize(w2_c, w2_s, w2_late, 0, N)
        add(0, half_v)
        add(half_v, half_v)
        for i in range(2):
            quantize(z_c, z_s, z_b, i * half_v, half_v)
        for i in range(2):
            sl = slice(i * half_v, (i + 1) * half_v)
            acc = banks[i]
            nc.tensor.matmul_mx(
                out=acc[:, :half_v],
                lhsT=w2_c[:].bitcast(FP8X4),
                lhsT_scale=w2_s[:],
                rhs=z_c[:, sl].bitcast(FP8X4),
                rhs_scale=z_s[:, sl],
                start=True,
                stop=True,
            )
            nc.scalar.copy(o_sb[:, sl], acc[:, :half_v])
            nc.sync.dma_start(out=out[:, sl], in_=o_sb[:, sl])
